import numpy as np
import ml_dtypes


def mxq(x, axis, fmt="e4m3"):
    dtype, down = {"e4m3": (ml_dtypes.float8_e4m3fn, 7), "e5m2": (ml_dtypes.float8_e5m2, 14)}[fmt]
    v = np.moveaxis(np.asarray(x, np.float32).astype(ml_dtypes.bfloat16).astype(np.float64), axis, -1)
    blocks = v.reshape(v.shape[:-1] + (-1, 32))
    amax = np.abs(blocks).max(-1, keepdims=True)
    byte = np.maximum(np.where(amax > 0, np.frexp(amax)[1] - 1 + 127, 0) - down, 1)
    scale = np.exp2(byte - 127.0)
    codes = (blocks / scale).astype(np.float32).astype(dtype).astype(np.float64)
    return np.moveaxis((codes * scale).reshape(v.shape), -1, axis)


WIDE = False


def mx_kscale(k):
    if not WIDE:
        return np.ones(k)
    levels = np.array([10, -10, 5, -5, 0])
    if k % 512:
        return np.exp2(np.random.permutation(np.resize(levels, k // 32))).repeat(32)
    a = np.empty((k // 512, 16))
    for p in range(k // 512):
        a[p, :8] = np.random.permutation(np.resize(levels, 8))
        for g in range(8):
            far = levels[np.abs(levels - a[p, g]) >= 10]
            a[p, g + 8] = far[np.random.randint(len(far))]
    return np.exp2(a.ravel()).repeat(32)


def f64(x):
    return np.asarray(x).astype(np.float64)


def split(x):
    m, e = np.frexp(f64(x))
    hi = np.ldexp(np.trunc(16.0 * m) / 16.0, e)
    return hi, f64(x) - hi


def silu(v):
    return v / (1.0 + np.exp(-np.maximum(v, -700.0)))


K, M, T = 1536, 512, 512


def setup_inputs():
    n = np.random.standard_normal
    s = mx_kscale(K)[:, None]
    return {
        "w": (n((K, M)) / np.sqrt(K) / s).astype(np.float32),
        "x": (n((K, T)) * s).astype(np.float32),
        "b": (0.3 * n(512)).astype(np.float32),
    }


def reference(w, x, b):
    w_hi, w_lo = split(w)
    w_hi_, w_lo_ = mxq(w_hi, 0, "e4m3"), mxq(w_lo, 0, "e4m3")
    x_ = mxq(f64(x), 0, "e4m3")
    y = w_hi_.T @ x_ + w_lo_.T @ x_
    return silu(y + f64(b)[:, None])

@@ -1,0 +1,245 @@
+from contextlib import ExitStack
+
+import concourse.mybir as mybir
+from concourse.masks import make_identity
+
+K, M, T = 1536, 512, 512
+FLOPS = 2 * 2 * K * M * T
+
+F32 = mybir.dt.float32
+BF16 = mybir.dt.bfloat16
+I32 = mybir.dt.int32
+U32 = mybir.dt.uint32
+U8 = mybir.dt.uint8
+FP8X4 = mybir.dt.float8_e4m3fn_x4
+ALU = mybir.AluOpType
+ACT = mybir.ActivationFunctionType
+
+P = 128
+PACK = 4
+K_PASS = P * PACK
+PASSES = K // K_PASS
+TILES = M // P
+
+HI_WORD = -1048576
+HI_PAIR = -983056
+HI_LOW_HALF = 0xFFF0
+
+
+def tile_mix_hilo_fm_silu_kernel(tc, w, x, b, out):
+    nc = tc.nc
+    with ExitStack() as ctx:
+        keep = ctx.enter_context(tc.tile_pool(name="keep", bufs=1))
+        psum = ctx.enter_context(tc.psum_pool(name="psum", bufs=1))
+
+        def keep_tile(name, shape, dtype):
+            t = keep.tile(shape, dtype, name=name, align_bytes=64)
+            return t
+
+        def per_pass(name, shape, dtype):
+            return [keep_tile(name + str(g), shape, dtype) for g in range(PASSES)]
+
+        w_raw = per_pass("w_raw", [P, PACK, M], F32)
+        x_raw = per_pass("x_raw", [P, PACK, T], F32)
+        w_top = per_pass("w_top", [P, M, PACK], BF16)
+        w_even = per_pass("w_even", [P, 2, M], I32)
+        w_hi = per_pass("w_hi", [P, M, 2], I32)
+        w_lo = per_pass("w_lo", [P, M, PACK], BF16)
+        x_bf = per_pass("x_bf", [P, T, PACK], BF16)
+        hi_codes = per_pass("hi_codes", [P, M], U32)
+        hi_scales = per_pass("hi_scales", [P, M], U8)
+        lo_codes = per_pass("lo_codes", [P, M], U32)
+        lo_scales = per_pass("lo_scales", [P, M], U8)
+        x_codes = per_pass("x_codes", [P, T], U32)
+        x_scales = per_pass("x_scales", [P, T], U8)
+        acc = [psum.tile([P, T], F32, name="acc" + str(m)) for m in range(TILES)]
+        res = [keep_tile("res" + str(m), [P, T], F32) for m in range(TILES)]
+
+        warm = keep_tile("warm", [P, 8], F32)
+        b_rows = keep_tile("b_rows", [P, P], F32)
+        b_cols = keep_tile("b_cols", [P, TILES], F32)
+        ident = keep_tile("ident", [P, P], F32)
+        b_turn = psum.tile([P, P], F32, name="b_turn")
+
+        def load(src, dst, g, c0, c1):
+            rows = src[g * K_PASS : (g + 1) * K_PASS, c0:c1]
+            nc.sync.dma_start(out=dst[g][:, :, c0:c1], in_=rows.rearrange("(p j) c -> p j c", j=PACK))
+
+        def grouped(t, g, c0, c1):
+            return t[g][:, c0:c1, :].rearrange("p (c i) t -> p c t i", i=4)
+
+        def by_row(t, g, c0, c1):
+            return t[g][:, :, c0:c1].rearrange("p t (c i) -> p c t i", i=4)
+
+        def top_halves(g, c0, c1):
+            halves = w_raw[g][:].bitcast(BF16)
+            nc.scalar.copy(
+                out=grouped(w_top, g, c0, c1),
+                in_=halves[:, :, 2 * c0 + 1 : 2 * c1 : 2].rearrange("p t (c i) -> p c t i", i=4),
+            )
+
+        def mask_top(g, c0, c1):
+            nc.vector.tensor_scalar(
+                out=w_hi[g][:, c0:c1, :].rearrange("p c u -> p (c u)"),
+                in0=w_top[g][:, c0:c1, :].rearrange("p c t -> p (c t)").bitcast(I32),
+                scalar1=HI_PAIR,
+                scalar2=None,
+                op0=ALU.bitwise_and,
+            )
+
+        def even_rows(g, c0, c1):
+            words = w_raw[g][:].bitcast(I32)
+            nc.vector.tensor_scalar(
+                out=w_even[g][:, :, c0:c1],
+                in0=words[:, 0:4:2, c0:c1],
+                scalar1=16,
+                scalar2=HI_LOW_HALF,
+                op0=ALU.logical_shift_right,
+                op1=ALU.bitwise_and,
+            )
+
+        def odd_rows(g, c0, c1):
+            words = w_raw[g][:].bitcast(I32)
+            nc.vector.scalar_tensor_tensor(
+                out=w_hi[g][:, c0:c1, :],
+                in0=words[:, 1:4:2, c0:c1].rearrange("p u c -> p c u"),
+                scalar=HI_WORD,
+                in1=w_even[g][:, :, c0:c1].rearrange("p u c -> p c u"),
+                op0=ALU.bitwise_and,
+                op1=ALU.bitwise_or,
+            )
+
+        def subtract(g, c0, c1):
+            hi = w_hi[g][:].rearrange("p c u -> p (c u)").bitcast(BF16)[:, PACK * c0 : PACK * c1]
+            nc.vector.tensor_tensor(
+                out=grouped(w_lo, g, c0, c1),
+                in0=by_row(w_raw, g, c0, c1),
+                in1=hi.rearrange("p (c i t) -> p c t i", i=4, t=PACK),
+                op=ALU.subtract,
+            )
+
+        def quantize(codes, scales, src, g, c0, c1):
+            nc.vector.quantize_mx(
+                out=codes[g][:, c0:c1].bitcast(FP8X4),
+                scales=scales[g][:, c0:c1],
+                in_=src,
+            )
+
+        def quantize_hi(g, c0, c1):
+            src = w_hi[g][:].rearrange("p c u -> p (c u)").bitcast(BF16)[:, PACK * c0 : PACK * c1]
+            quantize(hi_codes, hi_scales, src, g, c0, c1)
+
+        def quantize_lo(g, c0, c1):
+            quantize(lo_codes, lo_scales, w_lo[g][:].rearrange("p c t -> p (c t)")[:, PACK * c0 : PACK * c1], g, c0, c1)
+
+        def quantize_x(g, c0, c1):
+            quantize(x_codes, x_scales, x_bf[g][:].rearrange("p c t -> p (c t)")[:, PACK * c0 : PACK * c1], g, c0, c1)
+
+        def round_x(engine_copy, g, c0, c1):
+            engine_copy(out=grouped(x_bf, g, c0, c1), in_=by_row(x_raw, g, c0, c1))
+
+        def multiply(codes, scales, g, m, start=False, stop=False):
+            cols = slice(m * P, (m + 1) * P)
+            nc.tensor.matmul_mx(
+                out=acc[m][:],
+                lhsT=codes[g][:, cols].bitcast(FP8X4),
+                lhsT_scale=scales[g][:, cols],
+                rhs=x_codes[g][:].bitcast(FP8X4),
+                rhs_scale=x_scales[g][:],
+                start=start,
+                stop=stop,
+            )
+
+        def hi_pass(g, m):
+            multiply(hi_codes, hi_scales, g, m, start=(g == 0))
+
+        def lo_pass(g, m):
+            multiply(lo_codes, lo_scales, g, m, stop=(g == PASSES - 1))
+
+        def finish(m):
+            nc.scalar.activation(out=res[m][:], in_=acc[m][:], func=ACT.Silu, bias=b_cols[:, m : m + 1], scale=1.0)
+            nc.sync.dma_start(out=out[m * P : (m + 1) * P, :], in_=res[m][:])
+
+        with tc.manual_schedule():
+            load(w, w_raw, 0, 0, 128)
+            load(w, w_raw, 0, 128, 256)
+            load(w, w_raw, 0, 256, 512)
+            load(x, x_raw, 0, 0, 256)
+            load(x, x_raw, 0, 256, 512)
+            load(w, w_raw, 1, 0, 256)
+            load(w, w_raw, 1, 256, 512)
+            load(x, x_raw, 1, 0, 512)
+            load(w, w_raw, 2, 0, 256)
+            load(x, x_raw, 2, 0, 512)
+            load(w, w_raw, 2, 256, 512)
+
+            nc.vector.memset(b_rows[:], 0.0)
+            nc.vector.memset(warm[:], 0.0)
+            nc.scalar.dma_start(out=b_rows[0:TILES, :], in_=b.rearrange("(m p) -> m p", p=P))
+            nc.scalar.activation(out=warm[:, 4:8], in_=warm[:, 0:4], func=ACT.Silu)
+            make_identity(nc, ident[:])
+            nc.tensor.transpose(b_turn[:], b_rows[:], ident[:])
+
+            even_rows(0, 0, 128)
+            odd_rows(0, 0, 128)
+            top_halves(0, 128, 256)
+            top_halves(0, 256, 512)
+            subtract(0, 0, 128)
+            mask_top(0, 128, 256)
+            quantize_hi(0, 0, 128)
+            subtract(0, 128, 256)
+            quantize_lo(0, 0, 128)
+            quantize_hi(0, 128, 256)
+            mask_top(0, 256, 512)
+            quantize_lo(0, 128, 256)
+            subtract(0, 256, 512)
+            quantize_hi(0, 256, 512)
+            round_x(nc.scalar.copy, 0, 0, 256)
+            round_x(nc.scalar.copy, 0, 256, 512)
+            even_rows(1, 0, 256)
+            quantize_lo(0, 256, 512)
+            odd_rows(1, 0, 256)
+            quantize_x(0, 0, 512)
+            for m in range(TILES):
+                hi_pass(0, m)
+                lo_pass(0, m)
+
+            top_halves(1, 256, 512)
+            round_x(nc.scalar.copy, 1, 0, 256)
+            top_halves(2, 0, 256)
+            subtract(1, 0, 256)
+            quantize_hi(1, 0, 256)
+            mask_top(1, 256, 512)
+            quantize_lo(1, 0, 256)
+            subtract(1, 256, 512)
+            quantize_hi(1, 256, 512)
+            mask_top(2, 0, 256)
+            quantize_lo(1, 256, 512)
+            round_x(nc.scalar.copy, 1, 256, 512)
+            nc.scalar.copy(out=b_cols[:], in_=b_turn[:, 0:TILES])
+            subtract(2, 0, 256)
+            quantize_x(1, 0, 512)
+            for m in range(TILES):
+                hi_pass(1, m)
+                lo_pass(1, m)
+
+            round_x(nc.scalar.copy, 2, 0, 512)
+            quantize_hi(2, 0, 256)
+            even_rows(2, 256, 512)
+            quantize_lo(2, 0, 256)
+            odd_rows(2, 256, 512)
+            quantize_x(2, 0, 512)
+            quantize_hi(2, 256, 512)
+            for m in (0, 1):
+                hi_pass(2, m)
+                lo_pass(2, m)
+                finish(m)
+            hi_pass(2, 2)
+            hi_pass(2, 3)
+            subtract(2, 256, 384)
+            subtract(2, 384, 512)
+            quantize_lo(2, 256, 384)
+            quantize_lo(2, 384, 512)
+            for m in (2, 3):
+                lo_pass(2, m)
+                finish(m)

@@ -156,23 +156,21 @@ def tile_mix_hilo_fm_silu_kernel(tc, w, x, b, out):
         def lo_pass(g, m):
             multiply(lo_codes, lo_scales, g, m, stop=(g == PASSES - 1))
 
-        def finish(m):
-            nc.scalar.activation(out=res[m][:], in_=acc[m][:], func=ACT.Silu, bias=b_cols[:, m : m + 1], scale=1.0)
-            nc.sync.dma_start(out=out[m * P : (m + 1) * P, :], in_=res[m][:])
+        def finish(m, parts=1):
+            for c in range(parts):
+                cols = slice(c * T // parts, (c + 1) * T // parts)
+                nc.scalar.activation(out=res[m][:, cols], in_=acc[m][:, cols], func=ACT.Silu, bias=b_cols[:, m : m + 1], scale=1.0)
+                nc.sync.dma_start(out=out[m * P : (m + 1) * P, cols], in_=res[m][:, cols])
 
         with tc.manual_schedule():
             load(w, w_raw, 0, 0, 128)
-            load(w, w_raw, 0, 128, 256)
-            load(w, w_raw, 0, 256, 512)
-            load(x, x_raw, 0, 0, 256)
-            load(x, x_raw, 0, 256, 512)
-            load(w, w_raw, 1, 0, 256)
-            load(w, w_raw, 1, 256, 512)
+            load(w, w_raw, 0, 128, 512)
+            load(w, w_raw, 1, 0, 512)
+            load(x, x_raw, 0, 0, 512)
             load(x, x_raw, 1, 0, 512)
             load(w, w_raw, 2, 0, 256)
             load(x, x_raw, 2, 0, 512)
             load(w, w_raw, 2, 256, 512)
-
             nc.vector.memset(b_rows[:], 0.0)
             nc.vector.memset(warm[:], 0.0)
             nc.scalar.dma_start(out=b_rows[0:TILES, :], in_=b.rearrange("(m p) -> m p", p=P))
@@ -180,66 +178,71 @@ def tile_mix_hilo_fm_silu_kernel(tc, w, x, b, out):
             make_identity(nc, ident[:])
             nc.tensor.transpose(b_turn[:], b_rows[:], ident[:])
 
-            even_rows(0, 0, 128)
-            odd_rows(0, 0, 128)
+            top_halves(0, 0, 128)
             top_halves(0, 128, 256)
-            top_halves(0, 256, 512)
-            subtract(0, 0, 128)
-            mask_top(0, 128, 256)
+            mask_top(0, 0, 128)
             quantize_hi(0, 0, 128)
-            subtract(0, 128, 256)
+            subtract(0, 0, 128)
+            even_rows(0, 256, 512)
             quantize_lo(0, 0, 128)
-            quantize_hi(0, 128, 256)
-            mask_top(0, 256, 512)
-            quantize_lo(0, 128, 256)
+            odd_rows(0, 256, 512)
+            mask_top(0, 128, 256)
             subtract(0, 256, 512)
+            subtract(0, 128, 256)
             quantize_hi(0, 256, 512)
+            quantize_lo(0, 256, 512)
+            quantize_lo(0, 128, 256)
+
+            top_halves(1, 0, 256)
+            top_halves(1, 256, 512)
             round_x(nc.scalar.copy, 0, 0, 256)
             round_x(nc.scalar.copy, 0, 256, 512)
-            even_rows(1, 0, 256)
-            quantize_lo(0, 256, 512)
-            odd_rows(1, 0, 256)
-            quantize_x(0, 0, 512)
-            for m in range(TILES):
-                hi_pass(0, m)
-                lo_pass(0, m)
-
-            top_halves(1, 256, 512)
-            round_x(nc.scalar.copy, 1, 0, 256)
-            top_halves(2, 0, 256)
-            subtract(1, 0, 256)
+            nc.scalar.copy(out=b_cols[:], in_=b_turn[:, 0:TILES])
+            mask_top(1, 0, 256)
+            quantize_hi(0, 128, 256)
             quantize_hi(1, 0, 256)
+            subtract(1, 0, 256)
             mask_top(1, 256, 512)
             quantize_lo(1, 0, 256)
             subtract(1, 256, 512)
             quantize_hi(1, 256, 512)
-            mask_top(2, 0, 256)
+            quantize_x(0, 0, 512)
+            for m in range(TILES):
+                hi_pass(0, m)
+                lo_pass(0, m)
             quantize_lo(1, 256, 512)
+
+            round_x(nc.vector.tensor_copy, 1, 0, 256)
             round_x(nc.scalar.copy, 1, 256, 512)
-            nc.scalar.copy(out=b_cols[:], in_=b_turn[:, 0:TILES])
-            subtract(2, 0, 256)
+            top_halves(2, 0, 256)
+            round_x(nc.scalar.copy, 2, 0, 256)
+            round_x(nc.scalar.copy, 2, 256, 512)
+            top_halves(2, 256, 384)
+            top_halves(2, 384, 512)
+            mask_top(2, 0, 256)
             quantize_x(1, 0, 512)
             for m in range(TILES):
                 hi_pass(1, m)
                 lo_pass(1, m)
-
-            round_x(nc.scalar.copy, 2, 0, 512)
+            subtract(2, 0, 256)
             quantize_hi(2, 0, 256)
-            even_rows(2, 256, 512)
+            mask_top(2, 256, 384)
             quantize_lo(2, 0, 256)
-            odd_rows(2, 256, 512)
             quantize_x(2, 0, 512)
-            quantize_hi(2, 256, 512)
             for m in (0, 1):
                 hi_pass(2, m)
                 lo_pass(2, m)
                 finish(m)
-            hi_pass(2, 2)
-            hi_pass(2, 3)
             subtract(2, 256, 384)
+            mask_top(2, 384, 512)
+            quantize_hi(2, 256, 384)
+            hi_pass(2, 2)
             subtract(2, 384, 512)
             quantize_lo(2, 256, 384)
+            lo_pass(2, 2)
+            finish(2)
+            quantize_hi(2, 384, 512)
+            hi_pass(2, 3)
             quantize_lo(2, 384, 512)
-            for m in (2, 3):
-                lo_pass(2, m)
-                finish(m)
+            lo_pass(2, 3)
+            finish(3, 2)

@@ -19,11 +19,10 @@ P = 128
 PACK = 4
 K_PASS = P * PACK
 PASSES = K // K_PASS
+SIDE = 2
 TILES = M // P
 
-HI_WORD = -1048576
 HI_PAIR = -983056
-HI_LOW_HALF = 0xFFF0
 
 
 def tile_mix_hilo_fm_silu_kernel(tc, w, x, b, out):
@@ -42,7 +41,6 @@ def tile_mix_hilo_fm_silu_kernel(tc, w, x, b, out):
         w_raw = per_pass("w_raw", [P, PACK, M], F32)
         x_raw = per_pass("x_raw", [P, PACK, T], F32)
         w_top = per_pass("w_top", [P, M, PACK], BF16)
-        w_even = per_pass("w_even", [P, 2, M], I32)
         w_hi = per_pass("w_hi", [P, M, 2], I32)
         w_lo = per_pass("w_lo", [P, M, PACK], BF16)
         x_bf = per_pass("x_bf", [P, T, PACK], BF16)
@@ -61,21 +59,23 @@ def tile_mix_hilo_fm_silu_kernel(tc, w, x, b, out):
         ident = keep_tile("ident", [P, P], F32)
         b_turn = psum.tile([P, P], F32, name="b_turn")
 
+        on_scalar, on_vector = nc.scalar.copy, nc.vector.tensor_copy
+
         def load(src, dst, g, c0, c1):
             rows = src[g * K_PASS : (g + 1) * K_PASS, c0:c1]
             nc.sync.dma_start(out=dst[g][:, :, c0:c1], in_=rows.rearrange("(p j) c -> p j c", j=PACK))
 
         def grouped(t, g, c0, c1):
-            return t[g][:, c0:c1, :].rearrange("p (c i) t -> p c t i", i=4)
+            return t[g][:, c0:c1, :].rearrange("p (c i) t -> p c t i", i=SIDE)
 
         def by_row(t, g, c0, c1):
-            return t[g][:, :, c0:c1].rearrange("p t (c i) -> p c t i", i=4)
+            return t[g][:, :, c0:c1].rearrange("p t (c i) -> p c t i", i=SIDE)
 
-        def top_halves(g, c0, c1):
+        def top_halves(engine_copy, g, c0, c1):
             halves = w_raw[g][:].bitcast(BF16)
-            nc.scalar.copy(
+            engine_copy(
                 out=grouped(w_top, g, c0, c1),
-                in_=halves[:, :, 2 * c0 + 1 : 2 * c1 : 2].rearrange("p t (c i) -> p c t i", i=4),
+                in_=halves[:, :, 2 * c0 + 1 : 2 * c1 : 2].rearrange("p t (c i) -> p c t i", i=SIDE),
             )
 
         def mask_top(g, c0, c1):
@@ -87,34 +87,12 @@ def tile_mix_hilo_fm_silu_kernel(tc, w, x, b, out):
                 op0=ALU.bitwise_and,
             )
 
-        def even_rows(g, c0, c1):
-            words = w_raw[g][:].bitcast(I32)
-            nc.vector.tensor_scalar(
-                out=w_even[g][:, :, c0:c1],
-                in0=words[:, 0:4:2, c0:c1],
-                scalar1=16,
-                scalar2=HI_LOW_HALF,
-                op0=ALU.logical_shift_right,
-                op1=ALU.bitwise_and,
-            )
-
-        def odd_rows(g, c0, c1):
-            words = w_raw[g][:].bitcast(I32)
-            nc.vector.scalar_tensor_tensor(
-                out=w_hi[g][:, c0:c1, :],
-                in0=words[:, 1:4:2, c0:c1].rearrange("p u c -> p c u"),
-                scalar=HI_WORD,
-                in1=w_even[g][:, :, c0:c1].rearrange("p u c -> p c u"),
-                op0=ALU.bitwise_and,
-                op1=ALU.bitwise_or,
-            )
-
         def subtract(g, c0, c1):
             hi = w_hi[g][:].rearrange("p c u -> p (c u)").bitcast(BF16)[:, PACK * c0 : PACK * c1]
             nc.vector.tensor_tensor(
                 out=grouped(w_lo, g, c0, c1),
                 in0=by_row(w_raw, g, c0, c1),
-                in1=hi.rearrange("p (c i t) -> p c t i", i=4, t=PACK),
+                in1=hi.rearrange("p (c i t) -> p c t i", i=SIDE, t=PACK),
                 op=ALU.subtract,
             )
 
@@ -163,13 +141,14 @@ def tile_mix_hilo_fm_silu_kernel(tc, w, x, b, out):
                 nc.sync.dma_start(out=out[m * P : (m + 1) * P, cols], in_=res[m][:, cols])
 
         with tc.manual_schedule():
-            load(w, w_raw, 0, 0, 128)
-            load(w, w_raw, 0, 128, 512)
+            load(w, w_raw, 0, 0, 256)
+            load(w, w_raw, 0, 256, 512)
             load(w, w_raw, 1, 0, 512)
             load(x, x_raw, 0, 0, 512)
             load(x, x_raw, 1, 0, 512)
             load(w, w_raw, 2, 0, 256)
-            load(x, x_raw, 2, 0, 512)
+            load(x, x_raw, 2, 0, 256)
+            load(x, x_raw, 2, 256, 512)
             load(w, w_raw, 2, 256, 512)
             nc.vector.memset(b_rows[:], 0.0)
             nc.vector.memset(warm[:], 0.0)
@@ -178,47 +157,41 @@ def tile_mix_hilo_fm_silu_kernel(tc, w, x, b, out):
             make_identity(nc, ident[:])
             nc.tensor.transpose(b_turn[:], b_rows[:], ident[:])
 
-            top_halves(0, 0, 128)
-            top_halves(0, 128, 256)
-            mask_top(0, 0, 128)
-            quantize_hi(0, 0, 128)
-            subtract(0, 0, 128)
-            even_rows(0, 256, 512)
-            quantize_lo(0, 0, 128)
-            odd_rows(0, 256, 512)
-            mask_top(0, 128, 256)
+            top_halves(on_vector, 0, 0, 256)
+            top_halves(on_scalar, 0, 256, 512)
+            mask_top(0, 0, 256)
+            subtract(0, 0, 256)
+            quantize_hi(0, 0, 256)
+            mask_top(0, 256, 512)
+            quantize_lo(0, 0, 256)
             subtract(0, 256, 512)
-            subtract(0, 128, 256)
             quantize_hi(0, 256, 512)
-            quantize_lo(0, 256, 512)
-            quantize_lo(0, 128, 256)
 
-            top_halves(1, 0, 256)
-            top_halves(1, 256, 512)
-            round_x(nc.scalar.copy, 0, 0, 256)
-            round_x(nc.scalar.copy, 0, 256, 512)
-            nc.scalar.copy(out=b_cols[:], in_=b_turn[:, 0:TILES])
+            top_halves(on_scalar, 1, 0, 256)
+            top_halves(on_scalar, 1, 256, 512)
             mask_top(1, 0, 256)
-            quantize_hi(0, 128, 256)
+            quantize_lo(0, 256, 512)
             quantize_hi(1, 0, 256)
             subtract(1, 0, 256)
             mask_top(1, 256, 512)
             quantize_lo(1, 0, 256)
             subtract(1, 256, 512)
-            quantize_hi(1, 256, 512)
+            round_x(on_scalar, 0, 0, 512)
+            nc.scalar.copy(out=b_cols[:], in_=b_turn[:, 0:TILES])
             quantize_x(0, 0, 512)
             for m in range(TILES):
                 hi_pass(0, m)
                 lo_pass(0, m)
-            quantize_lo(1, 256, 512)
 
-            round_x(nc.vector.tensor_copy, 1, 0, 256)
-            round_x(nc.scalar.copy, 1, 256, 512)
-            top_halves(2, 0, 256)
-            round_x(nc.scalar.copy, 2, 0, 256)
-            round_x(nc.scalar.copy, 2, 256, 512)
-            top_halves(2, 256, 384)
-            top_halves(2, 384, 512)
+            round_x(on_scalar, 1, 0, 256)
+            round_x(on_scalar, 1, 256, 512)
+            round_x(on_scalar, 2, 0, 256)
+            round_x(on_scalar, 2, 256, 512)
+            top_halves(on_scalar, 2, 256, 384)
+            top_halves(on_scalar, 2, 384, 512)
+            quantize_lo(1, 256, 512)
+            top_halves(on_vector, 2, 0, 256)
+            quantize_hi(1, 256, 512)
             mask_top(2, 0, 256)
             quantize_x(1, 0, 512)
             for m in range(TILES):
@@ -226,21 +199,21 @@ def tile_mix_hilo_fm_silu_kernel(tc, w, x, b, out):
                 lo_pass(1, m)
             subtract(2, 0, 256)
             quantize_hi(2, 0, 256)
-            mask_top(2, 256, 384)
             quantize_lo(2, 0, 256)
             quantize_x(2, 0, 512)
             for m in (0, 1):
                 hi_pass(2, m)
                 lo_pass(2, m)
                 finish(m)
+            mask_top(2, 256, 384)
             subtract(2, 256, 384)
-            mask_top(2, 384, 512)
             quantize_hi(2, 256, 384)
-            hi_pass(2, 2)
-            subtract(2, 384, 512)
+            mask_top(2, 384, 512)
             quantize_lo(2, 256, 384)
+            hi_pass(2, 2)
             lo_pass(2, 2)
             finish(2)
+            subtract(2, 384, 512)
             quantize_hi(2, 384, 512)
             hi_pass(2, 3)
             quantize_lo(2, 384, 512)

@@ -19,10 +19,11 @@ P = 128
 PACK = 4
 K_PASS = P * PACK
 PASSES = K // K_PASS
-SIDE = 2
 TILES = M // P
 
+HI_WORD = -1048576
 HI_PAIR = -983056
+HI_LOW_HALF = 0xFFF0
 
 
 def tile_mix_hilo_fm_silu_kernel(tc, w, x, b, out):
@@ -41,6 +42,7 @@ def tile_mix_hilo_fm_silu_kernel(tc, w, x, b, out):
         w_raw = per_pass("w_raw", [P, PACK, M], F32)
         x_raw = per_pass("x_raw", [P, PACK, T], F32)
         w_top = per_pass("w_top", [P, M, PACK], BF16)
+        w_even = per_pass("w_even", [P, 2, M], I32)
         w_hi = per_pass("w_hi", [P, M, 2], I32)
         w_lo = per_pass("w_lo", [P, M, PACK], BF16)
         x_bf = per_pass("x_bf", [P, T, PACK], BF16)
@@ -59,23 +61,21 @@ def tile_mix_hilo_fm_silu_kernel(tc, w, x, b, out):
         ident = keep_tile("ident", [P, P], F32)
         b_turn = psum.tile([P, P], F32, name="b_turn")
 
-        on_scalar, on_vector = nc.scalar.copy, nc.vector.tensor_copy
-
         def load(src, dst, g, c0, c1):
             rows = src[g * K_PASS : (g + 1) * K_PASS, c0:c1]
             nc.sync.dma_start(out=dst[g][:, :, c0:c1], in_=rows.rearrange("(p j) c -> p j c", j=PACK))
 
         def grouped(t, g, c0, c1):
-            return t[g][:, c0:c1, :].rearrange("p (c i) t -> p c t i", i=SIDE)
+            return t[g][:, c0:c1, :].rearrange("p (c i) t -> p c t i", i=4)
 
         def by_row(t, g, c0, c1):
-            return t[g][:, :, c0:c1].rearrange("p t (c i) -> p c t i", i=SIDE)
+            return t[g][:, :, c0:c1].rearrange("p t (c i) -> p c t i", i=4)
 
-        def top_halves(engine_copy, g, c0, c1):
+        def top_halves(g, c0, c1):
             halves = w_raw[g][:].bitcast(BF16)
-            engine_copy(
+            nc.scalar.copy(
                 out=grouped(w_top, g, c0, c1),
-                in_=halves[:, :, 2 * c0 + 1 : 2 * c1 : 2].rearrange("p t (c i) -> p c t i", i=SIDE),
+                in_=halves[:, :, 2 * c0 + 1 : 2 * c1 : 2].rearrange("p t (c i) -> p c t i", i=4),
             )
 
         def mask_top(g, c0, c1):
@@ -87,12 +87,34 @@ def tile_mix_hilo_fm_silu_kernel(tc, w, x, b, out):
                 op0=ALU.bitwise_and,
             )
 
+        def even_rows(g, c0, c1):
+            words = w_raw[g][:].bitcast(I32)
+            nc.vector.tensor_scalar(
+                out=w_even[g][:, :, c0:c1],
+                in0=words[:, 0:4:2, c0:c1],
+                scalar1=16,
+                scalar2=HI_LOW_HALF,
+                op0=ALU.logical_shift_right,
+                op1=ALU.bitwise_and,
+            )
+
+        def odd_rows(g, c0, c1):
+            words = w_raw[g][:].bitcast(I32)
+            nc.vector.scalar_tensor_tensor(
+                out=w_hi[g][:, c0:c1, :],
+                in0=words[:, 1:4:2, c0:c1].rearrange("p u c -> p c u"),
+                scalar=HI_WORD,
+                in1=w_even[g][:, :, c0:c1].rearrange("p u c -> p c u"),
+                op0=ALU.bitwise_and,
+                op1=ALU.bitwise_or,
+            )
+
         def subtract(g, c0, c1):
             hi = w_hi[g][:].rearrange("p c u -> p (c u)").bitcast(BF16)[:, PACK * c0 : PACK * c1]
             nc.vector.tensor_tensor(
                 out=grouped(w_lo, g, c0, c1),
                 in0=by_row(w_raw, g, c0, c1),
-                in1=hi.rearrange("p (c i t) -> p c t i", i=SIDE, t=PACK),
+                in1=hi.rearrange("p (c i t) -> p c t i", i=4, t=PACK),
                 op=ALU.subtract,
             )
 
@@ -157,9 +179,9 @@ def tile_mix_hilo_fm_silu_kernel(tc, w, x, b, out):
             make_identity(nc, ident[:])
             nc.tensor.transpose(b_turn[:], b_rows[:], ident[:])
 
-            top_halves(on_vector, 0, 0, 256)
-            top_halves(on_scalar, 0, 256, 512)
-            mask_top(0, 0, 256)
+            even_rows(0, 0, 256)
+            top_halves(0, 256, 512)
+            odd_rows(0, 0, 256)
             subtract(0, 0, 256)
             quantize_hi(0, 0, 256)
             mask_top(0, 256, 512)
@@ -167,8 +189,8 @@ def tile_mix_hilo_fm_silu_kernel(tc, w, x, b, out):
             subtract(0, 256, 512)
             quantize_hi(0, 256, 512)
 
-            top_halves(on_scalar, 1, 0, 256)
-            top_halves(on_scalar, 1, 256, 512)
+            top_halves(1, 0, 256)
+            top_halves(1, 256, 512)
             mask_top(1, 0, 256)
             quantize_lo(0, 256, 512)
             quantize_hi(1, 0, 256)
@@ -176,23 +198,23 @@ def tile_mix_hilo_fm_silu_kernel(tc, w, x, b, out):
             mask_top(1, 256, 512)
             quantize_lo(1, 0, 256)
             subtract(1, 256, 512)
-            round_x(on_scalar, 0, 0, 512)
+            round_x(nc.scalar.copy, 0, 0, 512)
             nc.scalar.copy(out=b_cols[:], in_=b_turn[:, 0:TILES])
             quantize_x(0, 0, 512)
             for m in range(TILES):
                 hi_pass(0, m)
                 lo_pass(0, m)
 
-            round_x(on_scalar, 1, 0, 256)
-            round_x(on_scalar, 1, 256, 512)
-            round_x(on_scalar, 2, 0, 256)
-            round_x(on_scalar, 2, 256, 512)
-            top_halves(on_scalar, 2, 256, 384)
-            top_halves(on_scalar, 2, 384, 512)
+            round_x(nc.scalar.copy, 1, 0, 256)
+            round_x(nc.scalar.copy, 1, 256, 512)
+            round_x(nc.scalar.copy, 2, 0, 256)
+            round_x(nc.scalar.copy, 2, 256, 512)
+            top_halves(2, 256, 384)
+            top_halves(2, 384, 512)
             quantize_lo(1, 256, 512)
-            top_halves(on_vector, 2, 0, 256)
+            even_rows(2, 0, 256)
             quantize_hi(1, 256, 512)
-            mask_top(2, 0, 256)
+            odd_rows(2, 0, 256)
             quantize_x(1, 0, 512)
             for m in range(TILES):
                 hi_pass(1, m)

from contextlib import ExitStack

import concourse.mybir as mybir
from concourse.masks import make_identity

K, M, T = 1536, 512, 512
FLOPS = 2 * 2 * K * M * T

F32 = mybir.dt.float32
BF16 = mybir.dt.bfloat16
I32 = mybir.dt.int32
U32 = mybir.dt.uint32
U8 = mybir.dt.uint8
FP8X4 = mybir.dt.float8_e4m3fn_x4
ALU = mybir.AluOpType
ACT = mybir.ActivationFunctionType

P = 128
PACK = 4
K_PASS = P * PACK
PASSES = K // K_PASS
TILES = M // P

HI_WORD = -1048576
HI_PAIR = -983056
HI_LOW_HALF = 0xFFF0


def tile_mix_hilo_fm_silu_kernel(tc, w, x, b, out):
    nc = tc.nc
    with ExitStack() as ctx:
        keep = ctx.enter_context(tc.tile_pool(name="keep", bufs=1))
        psum = ctx.enter_context(tc.psum_pool(name="psum", bufs=1))

        def keep_tile(name, shape, dtype):
            t = keep.tile(shape, dtype, name=name, align_bytes=64)
            return t

        def per_pass(name, shape, dtype):
            return [keep_tile(name + str(g), shape, dtype) for g in range(PASSES)]

        w_raw = per_pass("w_raw", [P, PACK, M], F32)
        x_raw = per_pass("x_raw", [P, PACK, T], F32)
        w_top = per_pass("w_top", [P, M, PACK], BF16)
        w_even = per_pass("w_even", [P, 2, M], I32)
        w_hi = per_pass("w_hi", [P, M, 2], I32)
        w_lo = per_pass("w_lo", [P, M, PACK], BF16)
        x_bf = per_pass("x_bf", [P, T, PACK], BF16)
        hi_codes = per_pass("hi_codes", [P, M], U32)
        hi_scales = per_pass("hi_scales", [P, M], U8)
        lo_codes = per_pass("lo_codes", [P, M], U32)
        lo_scales = per_pass("lo_scales", [P, M], U8)
        x_codes = per_pass("x_codes", [P, T], U32)
        x_scales = per_pass("x_scales", [P, T], U8)
        acc = [psum.tile([P, T], F32, name="acc" + str(m)) for m in range(TILES)]
        res = [keep_tile("res" + str(m), [P, T], F32) for m in range(TILES)]

        warm = keep_tile("warm", [P, 8], F32)
        b_rows = keep_tile("b_rows", [P, P], F32)
        b_cols = keep_tile("b_cols", [P, TILES], F32)
        ident = keep_tile("ident", [P, P], F32)
        b_turn = psum.tile([P, P], F32, name="b_turn")

        def load(src, dst, g, c0, c1):
            rows = src[g * K_PASS : (g + 1) * K_PASS, c0:c1]
            nc.sync.dma_start(out=dst[g][:, :, c0:c1], in_=rows.rearrange("(p j) c -> p j c", j=PACK))

        def grouped(t, g, c0, c1):
            return t[g][:, c0:c1, :].rearrange("p (c i) t -> p c t i", i=4)

        def by_row(t, g, c0, c1):
            return t[g][:, :, c0:c1].rearrange("p t (c i) -> p c t i", i=4)

        def top_halves(g, c0, c1):
            halves = w_raw[g][:].bitcast(BF16)
            nc.scalar.copy(
                out=grouped(w_top, g, c0, c1),
                in_=halves[:, :, 2 * c0 + 1 : 2 * c1 : 2].rearrange("p t (c i) -> p c t i", i=4),
            )

        def mask_top(g, c0, c1):
            nc.vector.tensor_scalar(
                out=w_hi[g][:, c0:c1, :].rearrange("p c u -> p (c u)"),
                in0=w_top[g][:, c0:c1, :].rearrange("p c t -> p (c t)").bitcast(I32),
                scalar1=HI_PAIR,
                scalar2=None,
                op0=ALU.bitwise_and,
            )

        def even_rows(g, c0, c1):
            words = w_raw[g][:].bitcast(I32)
            nc.vector.tensor_scalar(
                out=w_even[g][:, :, c0:c1],
                in0=words[:, 0:4:2, c0:c1],
                scalar1=16,
                scalar2=HI_LOW_HALF,
                op0=ALU.logical_shift_right,
                op1=ALU.bitwise_and,
            )

        def odd_rows(g, c0, c1):
            words = w_raw[g][:].bitcast(I32)
            nc.vector.scalar_tensor_tensor(
                out=w_hi[g][:, c0:c1, :],
                in0=words[:, 1:4:2, c0:c1].rearrange("p u c -> p c u"),
                scalar=HI_WORD,
                in1=w_even[g][:, :, c0:c1].rearrange("p u c -> p c u"),
                op0=ALU.bitwise_and,
                op1=ALU.bitwise_or,
            )

        def subtract(g, c0, c1):
            hi = w_hi[g][:].rearrange("p c u -> p (c u)").bitcast(BF16)[:, PACK * c0 : PACK * c1]
            nc.vector.tensor_tensor(
                out=grouped(w_lo, g, c0, c1),
                in0=by_row(w_raw, g, c0, c1),
                in1=hi.rearrange("p (c i t) -> p c t i", i=4, t=PACK),
                op=ALU.subtract,
            )

        def quantize(codes, scales, src, g, c0, c1):
            nc.vector.quantize_mx(
                out=codes[g][:, c0:c1].bitcast(FP8X4),
                scales=scales[g][:, c0:c1],
                in_=src,
            )

        def quantize_hi(g, c0, c1):
            src = w_hi[g][:].rearrange("p c u -> p (c u)").bitcast(BF16)[:, PACK * c0 : PACK * c1]
            quantize(hi_codes, hi_scales, src, g, c0, c1)

        def quantize_lo(g, c0, c1):
            quantize(lo_codes, lo_scales, w_lo[g][:].rearrange("p c t -> p (c t)")[:, PACK * c0 : PACK * c1], g, c0, c1)

        def quantize_x(g, c0, c1):
            quantize(x_codes, x_scales, x_bf[g][:].rearrange("p c t -> p (c t)")[:, PACK * c0 : PACK * c1], g, c0, c1)

        def round_x(engine_copy, g, c0, c1):
            engine_copy(out=grouped(x_bf, g, c0, c1), in_=by_row(x_raw, g, c0, c1))

        def multiply(codes, scales, g, m, start=False, stop=False):
            cols = slice(m * P, (m + 1) * P)
            nc.tensor.matmul_mx(
                out=acc[m][:],
                lhsT=codes[g][:, cols].bitcast(FP8X4),
                lhsT_scale=scales[g][:, cols],
                rhs=x_codes[g][:].bitcast(FP8X4),
                rhs_scale=x_scales[g][:],
                start=start,
                stop=stop,
            )

        def hi_pass(g, m):
            multiply(hi_codes, hi_scales, g, m, start=(g == 0))

        def lo_pass(g, m):
            multiply(lo_codes, lo_scales, g, m, stop=(g == PASSES - 1))

        def finish(m, parts=1):
            for c in range(parts):
                cols = slice(c * T // parts, (c + 1) * T // parts)
                nc.scalar.activation(out=res[m][:, cols], in_=acc[m][:, cols], func=ACT.Silu, bias=b_cols[:, m : m + 1], scale=1.0)
                nc.sync.dma_start(out=out[m * P : (m + 1) * P, cols], in_=res[m][:, cols])

        with tc.manual_schedule():
            load(w, w_raw, 0, 0, 256)
            load(w, w_raw, 0, 256, 512)
            load(w, w_raw, 1, 0, 512)
            load(x, x_raw, 0, 0, 512)
            load(x, x_raw, 1, 0, 512)
            load(w, w_raw, 2, 0, 256)
            load(x, x_raw, 2, 0, 256)
            load(x, x_raw, 2, 256, 512)
            load(w, w_raw, 2, 256, 512)
            nc.vector.memset(b_rows[:], 0.0)
            nc.vector.memset(warm[:], 0.0)
            nc.scalar.dma_start(out=b_rows[0:TILES, :], in_=b.rearrange("(m p) -> m p", p=P))
            nc.scalar.activation(out=warm[:, 4:8], in_=warm[:, 0:4], func=ACT.Silu)
            make_identity(nc, ident[:])
            nc.tensor.transpose(b_turn[:], b_rows[:], ident[:])

            even_rows(0, 0, 256)
            top_halves(0, 256, 512)
            odd_rows(0, 0, 256)
            subtract(0, 0, 256)
            quantize_hi(0, 0, 256)
            mask_top(0, 256, 512)
            quantize_lo(0, 0, 256)
            subtract(0, 256, 512)
            quantize_hi(0, 256, 512)

            top_halves(1, 0, 256)
            top_halves(1, 256, 512)
            mask_top(1, 0, 256)
            quantize_lo(0, 256, 512)
            quantize_hi(1, 0, 256)
            subtract(1, 0, 256)
            mask_top(1, 256, 512)
            quantize_lo(1, 0, 256)
            subtract(1, 256, 512)
            round_x(nc.scalar.copy, 0, 0, 512)
            nc.scalar.copy(out=b_cols[:], in_=b_turn[:, 0:TILES])
            quantize_x(0, 0, 512)
            for m in range(TILES):
                hi_pass(0, m)
                lo_pass(0, m)

            round_x(nc.scalar.copy, 1, 0, 256)
            round_x(nc.scalar.copy, 1, 256, 512)
            round_x(nc.scalar.copy, 2, 0, 256)
            round_x(nc.scalar.copy, 2, 256, 512)
            top_halves(2, 256, 384)
            top_halves(2, 384, 512)
            quantize_lo(1, 256, 512)
            even_rows(2, 0, 256)
            quantize_hi(1, 256, 512)
            odd_rows(2, 0, 256)
            quantize_x(1, 0, 512)
            for m in range(TILES):
                hi_pass(1, m)
                lo_pass(1, m)
            subtract(2, 0, 256)
            quantize_hi(2, 0, 256)
            quantize_lo(2, 0, 256)
            quantize_x(2, 0, 512)
            for m in (0, 1):
                hi_pass(2, m)
                lo_pass(2, m)
                finish(m)
            mask_top(2, 256, 384)
            subtract(2, 256, 384)
            quantize_hi(2, 256, 384)
            mask_top(2, 384, 512)
            quantize_lo(2, 256, 384)
            hi_pass(2, 2)
            lo_pass(2, 2)
            finish(2)
            subtract(2, 384, 512)
            quantize_hi(2, 384, 512)
            hi_pass(2, 3)
            quantize_lo(2, 384, 512)
            lo_pass(2, 3)
            finish(3, 2)
